import numpy as np
import ml_dtypes


def mxq(x, axis, fmt="e4m3"):
    dtype, down = {"e4m3": (ml_dtypes.float8_e4m3fn, 7), "e5m2": (ml_dtypes.float8_e5m2, 14)}[fmt]
    v = np.moveaxis(np.asarray(x, np.float32).astype(ml_dtypes.bfloat16).astype(np.float64), axis, -1)
    blocks = v.reshape(v.shape[:-1] + (-1, 32))
    amax = np.abs(blocks).max(-1, keepdims=True)
    byte = np.maximum(np.where(amax > 0, np.frexp(amax)[1] - 1 + 127, 0) - down, 1)
    scale = np.exp2(byte - 127.0)
    codes = (blocks / scale).astype(np.float32).astype(dtype).astype(np.float64)
    return np.moveaxis((codes * scale).reshape(v.shape), -1, axis)


WIDE = False


def mx_kscale(k):
    if not WIDE:
        return np.ones(k)
    levels = np.array([10, -10, 5, -5, 0])
    if k % 512:
        return np.exp2(np.random.permutation(np.resize(levels, k // 32))).repeat(32)
    a = np.empty((k // 512, 16))
    for p in range(k // 512):
        a[p, :8] = np.random.permutation(np.resize(levels, 8))
        for g in range(8):
            far = levels[np.abs(levels - a[p, g]) >= 10]
            a[p, g + 8] = far[np.random.randint(len(far))]
    return np.exp2(a.ravel()).repeat(32)


def f64(x):
    return np.asarray(x).astype(np.float64)


def planes(y):
    n, m = y.shape
    v = y.astype(np.float32).astype(ml_dtypes.bfloat16).astype(np.float64).reshape(n // 32, 32, m)
    top = np.abs(v).max(1)
    byte = np.clip(np.where(top > 0, np.frexp(top)[1] - 1 + 127 - 7, 1), 1, 254)
    codes = (v * np.exp2(127.0 - byte)[:, None, :]).reshape(n, m).astype(np.float32).astype(ml_dtypes.float8_e4m3fn).view(np.uint8)
    words = codes.reshape(n // 512, 128, 4, m).transpose(0, 1, 3, 2)
    return np.ascontiguousarray(words), np.ascontiguousarray(byte.astype(np.uint8).reshape(n // 512, 16, m))


def split(x):
    m, e = np.frexp(f64(x))
    hi = np.ldexp(np.trunc(16.0 * m) / 16.0, e)
    return hi, f64(x) - hi


K, M, T = 1536, 512, 1024


def setup_inputs():
    n = np.random.standard_normal
    s = mx_kscale(K)[:, None]
    return {
        "w": (n((K, M)) / np.sqrt(K) / s).astype(np.float32),
        "x": (n((K, T)) * s).astype(np.float32),
    }


def reference(w, x):
    w_hi, w_lo = split(w)
    w_hi_, w_lo_ = mxq(w_hi, 0, "e4m3"), mxq(w_lo, 0, "e4m3")
    x_ = mxq(f64(x), 0, "e4m3")
    y = x_.T @ w_hi_ + x_.T @ w_lo_
    out_0 = y
    return (out_0,) + planes(out_0)

@@ -1,0 +1,267 @@
+from contextlib import ExitStack
+
+import concourse.mybir as mybir
+
+K, M, T = 1536, 512, 1024
+FLOPS = 2 * 2 * K * M * T
+
+F32 = mybir.dt.float32
+BF16 = mybir.dt.bfloat16
+I32 = mybir.dt.int32
+U32 = mybir.dt.uint32
+U8 = mybir.dt.uint8
+FP8X4 = mybir.dt.float8_e4m3fn_x4
+ALU = mybir.AluOpType
+
+P = 128
+PACK = 4
+K_PASS = P * PACK
+PASSES = K // K_PASS
+T_HALF = P * PACK
+HALVES = T // T_HALF
+N_HALF = M // 2
+HI_MASK = -983056
+
+
+def tile_mix_hilo_tm_pl_none_kernel(tc, w, x, out_0, out_1, out_2):
+    nc = tc.nc
+    with ExitStack() as ctx:
+        sb = ctx.enter_context(tc.tile_pool(name="sb", bufs=1))
+        psum = ctx.enter_context(tc.psum_pool(name="psum", bufs=1))
+        ctx.enter_context(tc.manual_schedule())
+
+        def tiles(name, count, shape, dtype):
+            return [sb.tile(shape, dtype, name="%s%d" % (name, i), align_bytes=64) for i in range(count)]
+
+        w_raw = tiles("w_raw", PASSES, [P, PACK, M], F32)
+        w_top = tiles("w_top", PASSES, [P, M, PACK], BF16)
+        w_hi = tiles("w_hi", PASSES, [P, M, PACK], BF16)
+        w_lo = tiles("w_lo", PASSES, [P, M, PACK], BF16)
+        hi_codes = tiles("hi_codes", PASSES, [P, M], U32)
+        hi_scales = tiles("hi_scales", PASSES, [P, M], U8)
+        lo_codes = tiles("lo_codes", PASSES, [P, M], U32)
+        lo_scales = tiles("lo_scales", PASSES, [P, M], U8)
+        x_raw = tiles("x_raw", HALVES * PASSES, [P, PACK, T_HALF], F32)
+        x_bf = tiles("x_bf", HALVES * PASSES, [P, PACK, P, PACK], BF16)
+        x_codes = tiles("x_codes", HALVES * PASSES, [P, T_HALF], U32)
+        x_scales = tiles("x_scales", HALVES * PASSES, [P, T_HALF], U8)
+        res = tiles("res", HALVES, [P, PACK, M], F32)
+        res_bf = tiles("res_bf", HALVES, [P, M, PACK], BF16)
+        res_codes = tiles("res_codes", HALVES, [P, M], U32)
+        res_scales = tiles("res_scales", HALVES, [P, M], U8)
+
+        def copy_on(engine, out, in_):
+            if engine == "S":
+                nc.scalar.copy(out=out, in_=in_)
+            else:
+                nc.vector.tensor_copy(out=out, in_=in_)
+
+        def load_w(g, n0, n1):
+            rows = w[g * K_PASS : (g + 1) * K_PASS, n0:n1]
+            nc.sync.dma_start(out=w_raw[g][:, :, n0:n1], in_=rows.rearrange("(p j) n -> p j n", j=PACK))
+
+        def load_x(a, g, t0, t1):
+            rows = x[g * K_PASS : (g + 1) * K_PASS, a * T_HALF + t0 : a * T_HALF + t1]
+            nc.sync.dma_start(
+                out=x_raw[a * PASSES + g][:, :, t0:t1], in_=rows.rearrange("(p j) t -> p j t", j=PACK)
+            )
+
+        def words_first(ap):
+            return ap.rearrange("p (c i) j -> p c j i", i=4)
+
+        def rows_first(ap):
+            return ap.rearrange("p j (c i) -> p c j i", i=4)
+
+        def top(g, n0, n1, engine):
+            upper = w_raw[g][:].bitcast(BF16)[:, :, 2 * n0 + 1 : 2 * n1 : 2]
+            copy_on(engine, words_first(w_top[g][:, n0:n1, :]), rows_first(upper))
+
+        def flat(ap):
+            return ap.rearrange("p n j -> p (n j)")
+
+        def mask(g, n0, n1):
+            nc.vector.tensor_scalar(
+                out=flat(w_hi[g][:, n0:n1, :]).bitcast(I32),
+                in0=flat(w_top[g][:, n0:n1, :]).bitcast(I32),
+                scalar1=HI_MASK,
+                scalar2=None,
+                op0=ALU.bitwise_and,
+            )
+
+        def sub(g, n0, n1):
+            nc.vector.tensor_tensor(
+                out=words_first(w_lo[g][:, n0:n1, :]),
+                in0=rows_first(w_raw[g][:, :, n0:n1]),
+                in1=words_first(w_hi[g][:, n0:n1, :]),
+                op=ALU.subtract,
+            )
+
+        def quantize(codes, scales, values, c0, c1):
+            nc.vector.quantize_mx(
+                out=codes[:, c0:c1].bitcast(FP8X4), scales=scales[:, c0:c1], in_=values[:, PACK * c0 : PACK * c1]
+            )
+
+        def quantize_hi(g, n0, n1):
+            quantize(hi_codes[g], hi_scales[g], flat(w_hi[g][:]), n0, n1)
+
+        def quantize_lo(g, n0, n1):
+            quantize(lo_codes[g], lo_scales[g], flat(w_lo[g][:]), n0, n1)
+
+        def cast(a, g, m0, m1, engine):
+            i = a * PASSES + g
+            copy_on(
+                engine,
+                x_bf[i][:, :, m0:m1, :].rearrange("p r m j -> p m j r"),
+                x_raw[i][:, :, PACK * m0 : PACK * m1].rearrange("p j (m r) -> p m j r", r=PACK),
+            )
+
+        def quantize_x(a, g, r0, r1):
+            i = a * PASSES + g
+            quantize(x_codes[i], x_scales[i], x_bf[i][:].rearrange("p r m j -> p (r m j)"), P * r0, P * r1)
+
+        acc = {}
+
+        def product(a, g, r, part):
+            i = a * PASSES + g
+            codes, scales = (hi_codes, hi_scales) if part == 0 else (lo_codes, lo_scales)
+            if g == 0 and part == 0:
+                acc[a, r] = psum.tile([P, M], F32, name="bank%d" % (PACK * a + r))
+            nc.tensor.matmul_mx(
+                out=acc[a, r][:],
+                lhsT=x_codes[i][:, P * r : P * (r + 1)].bitcast(FP8X4),
+                lhsT_scale=x_scales[i][:, P * r : P * (r + 1)],
+                rhs=codes[g][:].bitcast(FP8X4),
+                rhs_scale=scales[g][:],
+                start=(g == 0 and part == 0),
+                stop=(g == PASSES - 1 and part == 1),
+            )
+
+        def drain(a, r, n0, n1, engine):
+            copy_on(engine, res[a][:, r, n0:n1], acc[a, r][:, n0:n1])
+
+        def store_values(a, r):
+            rows = out_0[a * T_HALF : (a + 1) * T_HALF, :]
+            nc.sync.dma_start(out=rows.rearrange("(p r) n -> p r n", r=PACK)[:, r, :], in_=res[a][:, r, :])
+
+        def interleave(a, n0, n1, engine):
+            copy_on(engine, words_first(res_bf[a][:, n0:n1, :]), rows_first(res[a][:, :, n0:n1]))
+
+        def quantize_res(a, n0, n1):
+            quantize(res_codes[a], res_scales[a], flat(res_bf[a][:]), n0, n1)
+
+        def store_words(a, n0, n1, queue):
+            dst = out_1[a].rearrange("p n i -> p (n i)").bitcast(I32)
+            queue.dma_start(out=dst[:, n0:n1], in_=res_codes[a][:, n0:n1].bitcast(I32))
+
+        def store_scales(a, q, queue):
+            queue.dma_start(
+                out=out_2[a, 4 * q : 4 * q + 4, :].bitcast(I32),
+                in_=res_scales[a][32 * q : 32 * q + 4, :].bitcast(I32),
+            )
+
+        def products(a, g):
+            for part in range(2):
+                for r in range(PACK):
+                    product(a, g, r, part)
+
+        def products_by_bank(a, g):
+            for r in range(PACK):
+                for part in range(2):
+                    product(a, g, r, part)
+
+        H, Q, C = N_HALF, N_HALF // 2, 96
+        load_w(0, 0, Q)
+        load_w(0, Q, H)
+        load_w(0, H, M)
+        load_x(0, 0, 0, T_HALF)
+        load_w(1, 0, M)
+        load_x(0, 1, 0, T_HALF)
+        load_w(2, 0, M)
+        load_x(1, 0, 0, T_HALF)
+        load_x(0, 2, 0, T_HALF)
+        load_x(1, 1, 0, T_HALF)
+        load_x(1, 2, 0, 384)
+        load_x(1, 2, 384, T_HALF)
+
+        top(0, 0, Q, "V")
+        top(0, Q, H, "S")
+        top(0, H, M, "S")
+        mask(0, 0, Q)
+        sub(0, 0, Q)
+        mask(0, Q, H)
+        sub(0, Q, H)
+        quantize_hi(0, 0, H)
+        mask(0, H, M)
+        quantize_lo(0, 0, H)
+        sub(0, H, M)
+        cast(0, 0, 0, C, "S")
+        cast(0, 0, C, P, "V")
+        quantize_hi(0, H, M)
+        quantize_lo(0, H, M)
+        top(1, 0, H, "V")
+        top(1, H, M, "S")
+        quantize_x(0, 0, 0, PACK)
+        products(0, 0)
+        mask(1, 0, H)
+        mask(1, H, M)
+        sub(1, 0, H)
+        quantize_hi(1, 0, M)
+        cast(0, 1, 0, C, "S")
+        cast(0, 1, C, P, "V")
+        sub(1, H, M)
+        quantize_x(0, 1, 0, PACK)
+        quantize_lo(1, 0, M)
+        products(0, 1)
+        top(2, 0, H, "S")
+        top(2, H, M, "S")
+        mask(2, 0, H)
+        sub(2, 0, H)
+        cast(1, 0, 0, C, "S")
+        cast(1, 0, C, P, "V")
+        mask(2, H, M)
+        quantize_lo(2, 0, H)
+        quantize_x(1, 0, 0, PACK)
+        products(1, 0)
+        quantize_hi(2, 0, M)
+        cast(0, 2, 0, C, "S")
+        cast(0, 2, C, P, "V")
+        sub(2, H, M)
+        quantize_x(0, 2, 0, PACK)
+        quantize_lo(2, H, M)
+        products(0, 2)
+        cast(1, 1, 0, 64, "S")
+        cast(1, 1, 64, P, "V")
+        cast(1, 2, 0, 32, "S")
+        cast(1, 2, 32, C, "V")
+        quantize_x(1, 1, 0, PACK)
+        products(1, 1)
+        for r in range(PACK):
+            drain(0, r, 0, M, "S")
+            store_values(0, r)
+        cast(1, 2, C, P, "V")
+        quantize_x(1, 2, 0, 2)
+        quantize_x(1, 2, 2, PACK)
+        products_by_bank(1, 2)
+        interleave(0, 0, H, "V")
+        interleave(0, H, M, "V")
+        quantize_res(0, 0, M)
+        for r in range(2):
+            drain(1, r, 0, M, "S")
+            store_values(1, r)
+        store_words(0, 0, M, nc.sync)
+        for q in range(4):
+            store_scales(0, q, nc.sync)
+        drain(1, 2, 0, M, "S")
+        store_values(1, 2)
+        drain(1, 3, 0, H, "S")
+        drain(1, 3, H, M, "S")
+        store_values(1, 3)
+        interleave(1, 0, H, "V")
+        interleave(1, H + Q, M, "S")
+        interleave(1, H, H + Q, "V")
+        quantize_res(1, 0, H)
+        store_words(1, 0, H, nc.sync)
+        quantize_res(1, H, M)
+        store_words(1, H, M, nc.scalar)
+        for q in range(4):
+            store_scales(1, q, nc.scalar if q % 2 else nc.sync)

@@ -33,7 +33,15 @@ def tile_mix_hilo_tm_pl_none_kernel(tc, w, x, out_0, out_1, out_2):
         def tiles(name, count, shape, dtype):
             return [sb.tile(shape, dtype, name="%s%d" % (name, i), align_bytes=64) for i in range(count)]
 
-        w_raw = tiles("w_raw", PASSES, [P, PACK, M], F32)
+        w_first = tiles("w_first", 2, [P, PACK, N_HALF], F32)
+        w_later = tiles("w_later", PASSES - 1, [P, PACK, M], F32)
+
+        def w_raw(g, n0, n1):
+            if g > 0:
+                return w_later[g - 1][:, :, n0:n1]
+            h = n0 // N_HALF
+            return w_first[h][:, :, n0 - h * N_HALF : n1 - h * N_HALF]
+
         w_top = tiles("w_top", PASSES, [P, M, PACK], BF16)
         w_hi = tiles("w_hi", PASSES, [P, M, PACK], BF16)
         w_lo = tiles("w_lo", PASSES, [P, M, PACK], BF16)
@@ -41,14 +49,18 @@ def tile_mix_hilo_tm_pl_none_kernel(tc, w, x, out_0, out_1, out_2):
         hi_scales = tiles("hi_scales", PASSES, [P, M], U8)
         lo_codes = tiles("lo_codes", PASSES, [P, M], U32)
         lo_scales = tiles("lo_scales", PASSES, [P, M], U8)
-        x_raw = tiles("x_raw", HALVES * PASSES, [P, PACK, T_HALF], F32)
+        x_first = sb.tile([P, PACK, T], F32, name="x_first", align_bytes=64)
+        x_raw = {(a, 0): x_first[:, :, a * T_HALF : (a + 1) * T_HALF] for a in range(HALVES)}
+        for a in range(HALVES):
+            for g in range(1, PASSES):
+                x_raw[a, g] = sb.tile([P, PACK, T_HALF], F32, name="x_raw%d%d" % (a, g), align_bytes=64)[:]
         x_bf = tiles("x_bf", HALVES * PASSES, [P, PACK, P, PACK], BF16)
         x_codes = tiles("x_codes", HALVES * PASSES, [P, T_HALF], U32)
         x_scales = tiles("x_scales", HALVES * PASSES, [P, T_HALF], U8)
         res = tiles("res", HALVES, [P, PACK, M], F32)
         res_bf = tiles("res_bf", HALVES, [P, M, PACK], BF16)
         res_codes = tiles("res_codes", HALVES, [P, M], U32)
-        res_scales = tiles("res_scales", HALVES, [P, M], U8)
+        res_scales = sb.tile([P, HALVES, M], U8, name="res_scales", align_bytes=64)
 
         def copy_on(engine, out, in_):
             if engine == "S":
@@ -58,13 +70,11 @@ def tile_mix_hilo_tm_pl_none_kernel(tc, w, x, out_0, out_1, out_2):
 
         def load_w(g, n0, n1):
             rows = w[g * K_PASS : (g + 1) * K_PASS, n0:n1]
-            nc.sync.dma_start(out=w_raw[g][:, :, n0:n1], in_=rows.rearrange("(p j) n -> p j n", j=PACK))
+            nc.sync.dma_start(out=w_raw(g, n0, n1), in_=rows.rearrange("(p j) n -> p j n", j=PACK))
 
-        def load_x(a, g, t0, t1):
-            rows = x[g * K_PASS : (g + 1) * K_PASS, a * T_HALF + t0 : a * T_HALF + t1]
-            nc.sync.dma_start(
-                out=x_raw[a * PASSES + g][:, :, t0:t1], in_=rows.rearrange("(p j) t -> p j t", j=PACK)
-            )
+        def load_x(g, t0, t1, dst):
+            rows = x[g * K_PASS : (g + 1) * K_PASS, t0:t1]
+            nc.sync.dma_start(out=dst, in_=rows.rearrange("(p j) t -> p j t", j=PACK))
 
         def words_first(ap):
             return ap.rearrange("p (c i) j -> p c j i", i=4)
@@ -73,7 +83,7 @@ def tile_mix_hilo_tm_pl_none_kernel(tc, w, x, out_0, out_1, out_2):
             return ap.rearrange("p j (c i) -> p c j i", i=4)
 
         def top(g, n0, n1, engine):
-            upper = w_raw[g][:].bitcast(BF16)[:, :, 2 * n0 + 1 : 2 * n1 : 2]
+            upper = w_raw(g, n0, n1).bitcast(BF16)[:, :, 1 : 2 * (n1 - n0) : 2]
             copy_on(engine, words_first(w_top[g][:, n0:n1, :]), rows_first(upper))
 
         def flat(ap):
@@ -91,7 +101,7 @@ def tile_mix_hilo_tm_pl_none_kernel(tc, w, x, out_0, out_1, out_2):
         def sub(g, n0, n1):
             nc.vector.tensor_tensor(
                 out=words_first(w_lo[g][:, n0:n1, :]),
-                in0=rows_first(w_raw[g][:, :, n0:n1]),
+                in0=rows_first(w_raw(g, n0, n1)),
                 in1=words_first(w_hi[g][:, n0:n1, :]),
                 op=ALU.subtract,
             )
@@ -112,7 +122,7 @@ def tile_mix_hilo_tm_pl_none_kernel(tc, w, x, out_0, out_1, out_2):
             copy_on(
                 engine,
                 x_bf[i][:, :, m0:m1, :].rearrange("p r m j -> p m j r"),
-                x_raw[i][:, :, PACK * m0 : PACK * m1].rearrange("p j (m r) -> p m j r", r=PACK),
+                x_raw[a, g][:, :, PACK * m0 : PACK * m1].rearrange("p j (m r) -> p m j r", r=PACK),
             )
 
         def quantize_x(a, g, r0, r1):
@@ -139,24 +149,24 @@ def tile_mix_hilo_tm_pl_none_kernel(tc, w, x, out_0, out_1, out_2):
         def drain(a, r, n0, n1, engine):
             copy_on(engine, res[a][:, r, n0:n1], acc[a, r][:, n0:n1])
 
-        def store_values(a, r):
+        def store_values(a, r0, r1):
             rows = out_0[a * T_HALF : (a + 1) * T_HALF, :]
-            nc.sync.dma_start(out=rows.rearrange("(p r) n -> p r n", r=PACK)[:, r, :], in_=res[a][:, r, :])
+            nc.sync.dma_start(out=rows.rearrange("(p r) n -> p r n", r=PACK)[:, r0:r1, :], in_=res[a][:, r0:r1, :])
 
         def interleave(a, n0, n1, engine):
             copy_on(engine, words_first(res_bf[a][:, n0:n1, :]), rows_first(res[a][:, :, n0:n1]))
 
         def quantize_res(a, n0, n1):
-            quantize(res_codes[a], res_scales[a], flat(res_bf[a][:]), n0, n1)
+            quantize(res_codes[a], res_scales[:, a, :], flat(res_bf[a][:]), n0, n1)
 
         def store_words(a, n0, n1, queue):
             dst = out_1[a].rearrange("p n i -> p (n i)").bitcast(I32)
             queue.dma_start(out=dst[:, n0:n1], in_=res_codes[a][:, n0:n1].bitcast(I32))
 
-        def store_scales(a, q, queue):
+        def store_scales(q, queue):
             queue.dma_start(
-                out=out_2[a, 4 * q : 4 * q + 4, :].bitcast(I32),
-                in_=res_scales[a][32 * q : 32 * q + 4, :].bitcast(I32),
+                out=out_2[:, 4 * q : 4 * q + 4, :].rearrange("a r n -> r a n").bitcast(I32),
+                in_=res_scales[32 * q : 32 * q + 4, :, :].bitcast(I32),
             )
 
         def products(a, g):
@@ -169,99 +179,99 @@ def tile_mix_hilo_tm_pl_none_kernel(tc, w, x, out_0, out_1, out_2):
                 for part in range(2):
                     product(a, g, r, part)
 
-        H, Q, C = N_HALF, N_HALF // 2, 96
-        load_w(0, 0, Q)
-        load_w(0, Q, H)
+        H, Q = N_HALF, N_HALF // 2
+        load_w(0, 0, H)
         load_w(0, H, M)
-        load_x(0, 0, 0, T_HALF)
         load_w(1, 0, M)
-        load_x(0, 1, 0, T_HALF)
+        load_x(0, 0, T, x_first[:])
         load_w(2, 0, M)
-        load_x(1, 0, 0, T_HALF)
-        load_x(0, 2, 0, T_HALF)
-        load_x(1, 1, 0, T_HALF)
-        load_x(1, 2, 0, 384)
-        load_x(1, 2, 384, T_HALF)
+        load_x(1, 0, T_HALF, x_raw[0, 1])
+        load_x(2, 0, T_HALF, x_raw[0, 2])
+        load_x(1, T_HALF, T, x_raw[1, 1])
+        load_x(2, T_HALF, T, x_raw[1, 2])
 
         top(0, 0, Q, "V")
         top(0, Q, H, "S")
         top(0, H, M, "S")
         mask(0, 0, Q)
-        sub(0, 0, Q)
         mask(0, Q, H)
-        sub(0, Q, H)
+        sub(0, 0, Q)
         quantize_hi(0, 0, H)
+        sub(0, Q, H)
         mask(0, H, M)
         quantize_lo(0, 0, H)
         sub(0, H, M)
-        cast(0, 0, 0, C, "S")
-        cast(0, 0, C, P, "V")
-        quantize_hi(0, H, M)
-        quantize_lo(0, H, M)
-        top(1, 0, H, "V")
+        top(1, 0, H, "S")
         top(1, H, M, "S")
+        quantize_hi(0, H, M)
+        mask(1, 0, H)
+        quantize_lo(0, H, M)
+        sub(1, 0, H)
+        mask(1, H, M)
+        quantize_lo(1, 0, H)
+        quantize_hi(1, 0, H)
+        cast(0, 0, 0, 48, "S")
+        cast(0, 0, 48, P, "V")
+        cast(1, 0, 0, P, "S")
+        quantize_hi(1, H, M)
         quantize_x(0, 0, 0, PACK)
         products(0, 0)
-        mask(1, 0, H)
-        mask(1, H, M)
-        sub(1, 0, H)
-        quantize_hi(1, 0, M)
-        cast(0, 1, 0, C, "S")
-        cast(0, 1, C, P, "V")
         sub(1, H, M)
-        quantize_x(0, 1, 0, PACK)
-        quantize_lo(1, 0, M)
-        products(0, 1)
-        top(2, 0, H, "S")
+        top(2, 0, H, "V")
         top(2, H, M, "S")
+        quantize_lo(1, H, M)
         mask(2, 0, H)
-        sub(2, 0, H)
-        cast(1, 0, 0, C, "S")
-        cast(1, 0, C, P, "V")
-        mask(2, H, M)
-        quantize_lo(2, 0, H)
         quantize_x(1, 0, 0, PACK)
         products(1, 0)
+        sub(2, 0, H)
+        mask(2, H, M)
+        cast(0, 1, 0, 112, "S")
+        cast(0, 1, 112, P, "V")
         quantize_hi(2, 0, M)
-        cast(0, 2, 0, C, "S")
-        cast(0, 2, C, P, "V")
+        quantize_x(0, 1, 0, PACK)
+        products(0, 1)
+        cast(0, 2, 0, 112, "S")
+        cast(0, 2, 112, P, "V")
         sub(2, H, M)
         quantize_x(0, 2, 0, PACK)
-        quantize_lo(2, H, M)
-        products(0, 2)
-        cast(1, 1, 0, 64, "S")
-        cast(1, 1, 64, P, "V")
-        cast(1, 2, 0, 32, "S")
-        cast(1, 2, 32, C, "V")
+        quantize_lo(2, 0, M)
+        for r0 in (0, 2):
+            for part in range(2):
+                for r in (r0, r0 + 1):
+                    product(0, 2, r, part)
+        cast(1, 1, 0, 80, "S")
+        cast(1, 1, 80, P, "V")
         quantize_x(1, 1, 0, PACK)
         products(1, 1)
-        for r in range(PACK):
-            drain(0, r, 0, M, "S")
-            store_values(0, r)
-        cast(1, 2, C, P, "V")
+        drain(0, 0, 0, M, "S")
+        store_values(0, 0, 1)
+        drain(0, 1, 0, M, "S")
+        store_values(0, 1, 2)
+        drain(0, 2, 0, M, "S")
+        drain(0, 3, 0, M, "S")
+        store_values(0, 2, PACK)
+        cast(1, 2, 0, P, "V")
+        interleave(0, 0, H, "S")
         quantize_x(1, 2, 0, 2)
         quantize_x(1, 2, 2, PACK)
         products_by_bank(1, 2)
-        interleave(0, 0, H, "V")
         interleave(0, H, M, "V")
         quantize_res(0, 0, M)
-        for r in range(2):
-            drain(1, r, 0, M, "S")
-            store_values(1, r)
         store_words(0, 0, M, nc.sync)
-        for q in range(4):
-            store_scales(0, q, nc.sync)
+        drain(1, 0, 0, M, "S")
+        store_values(1, 0, 1)
+        drain(1, 1, 0, M, "V")
         drain(1, 2, 0, M, "S")
-        store_values(1, 2)
-        drain(1, 3, 0, H, "S")
+        store_values(1, 1, 3)
+        drain(1, 3, 0, H, "V")
         drain(1, 3, H, M, "S")
-        store_values(1, 3)
+        store_values(1, 3, PACK)
         interleave(1, 0, H, "V")
         interleave(1, H + Q, M, "S")
         interleave(1, H, H + Q, "V")
         quantize_res(1, 0, H)
-        store_words(1, 0, H, nc.sync)
+        store_words(1, 0, H, nc.scalar)
         quantize_res(1, H, M)
-        store_words(1, H, M, nc.scalar)
+        store_words(1, H, M, nc.sync)
         for q in range(4):
-            store_scales(1, q, nc.scalar if q % 2 else nc.sync)
+            store_scales(q, nc.sync if q % 2 else nc.scalar)

from contextlib import ExitStack

import concourse.mybir as mybir

K, M, T = 1536, 512, 1024
FLOPS = 2 * 2 * K * M * T

F32 = mybir.dt.float32
BF16 = mybir.dt.bfloat16
I32 = mybir.dt.int32
U32 = mybir.dt.uint32
U8 = mybir.dt.uint8
FP8X4 = mybir.dt.float8_e4m3fn_x4
ALU = mybir.AluOpType

P = 128
PACK = 4
K_PASS = P * PACK
PASSES = K // K_PASS
T_HALF = P * PACK
HALVES = T // T_HALF
N_HALF = M // 2
HI_MASK = -983056


def tile_mix_hilo_tm_pl_none_kernel(tc, w, x, out_0, out_1, out_2):
    nc = tc.nc
    with ExitStack() as ctx:
        sb = ctx.enter_context(tc.tile_pool(name="sb", bufs=1))
        psum = ctx.enter_context(tc.psum_pool(name="psum", bufs=1))
        ctx.enter_context(tc.manual_schedule())

        def tiles(name, count, shape, dtype):
            return [sb.tile(shape, dtype, name="%s%d" % (name, i), align_bytes=64) for i in range(count)]

        w_first = tiles("w_first", 2, [P, PACK, N_HALF], F32)
        w_later = tiles("w_later", PASSES - 1, [P, PACK, M], F32)

        def w_raw(g, n0, n1):
            if g > 0:
                return w_later[g - 1][:, :, n0:n1]
            h = n0 // N_HALF
            return w_first[h][:, :, n0 - h * N_HALF : n1 - h * N_HALF]

        w_top = tiles("w_top", PASSES, [P, M, PACK], BF16)
        w_hi = tiles("w_hi", PASSES, [P, M, PACK], BF16)
        w_lo = tiles("w_lo", PASSES, [P, M, PACK], BF16)
        hi_codes = tiles("hi_codes", PASSES, [P, M], U32)
        hi_scales = tiles("hi_scales", PASSES, [P, M], U8)
        lo_codes = tiles("lo_codes", PASSES, [P, M], U32)
        lo_scales = tiles("lo_scales", PASSES, [P, M], U8)
        x_first = sb.tile([P, PACK, T], F32, name="x_first", align_bytes=64)
        x_raw = {(a, 0): x_first[:, :, a * T_HALF : (a + 1) * T_HALF] for a in range(HALVES)}
        for a in range(HALVES):
            for g in range(1, PASSES):
                x_raw[a, g] = sb.tile([P, PACK, T_HALF], F32, name="x_raw%d%d" % (a, g), align_bytes=64)[:]
        x_bf = tiles("x_bf", HALVES * PASSES, [P, PACK, P, PACK], BF16)
        x_codes = tiles("x_codes", HALVES * PASSES, [P, T_HALF], U32)
        x_scales = tiles("x_scales", HALVES * PASSES, [P, T_HALF], U8)
        res = tiles("res", HALVES, [P, PACK, M], F32)
        res_bf = tiles("res_bf", HALVES, [P, M, PACK], BF16)
        res_codes = tiles("res_codes", HALVES, [P, M], U32)
        res_scales = sb.tile([P, HALVES, M], U8, name="res_scales", align_bytes=64)

        def copy_on(engine, out, in_):
            if engine == "S":
                nc.scalar.copy(out=out, in_=in_)
            else:
                nc.vector.tensor_copy(out=out, in_=in_)

        def load_w(g, n0, n1):
            rows = w[g * K_PASS : (g + 1) * K_PASS, n0:n1]
            nc.sync.dma_start(out=w_raw(g, n0, n1), in_=rows.rearrange("(p j) n -> p j n", j=PACK))

        def load_x(g, t0, t1, dst):
            rows = x[g * K_PASS : (g + 1) * K_PASS, t0:t1]
            nc.sync.dma_start(out=dst, in_=rows.rearrange("(p j) t -> p j t", j=PACK))

        def words_first(ap):
            return ap.rearrange("p (c i) j -> p c j i", i=4)

        def rows_first(ap):
            return ap.rearrange("p j (c i) -> p c j i", i=4)

        def top(g, n0, n1, engine):
            upper = w_raw(g, n0, n1).bitcast(BF16)[:, :, 1 : 2 * (n1 - n0) : 2]
            copy_on(engine, words_first(w_top[g][:, n0:n1, :]), rows_first(upper))

        def flat(ap):
            return ap.rearrange("p n j -> p (n j)")

        def mask(g, n0, n1):
            nc.vector.tensor_scalar(
                out=flat(w_hi[g][:, n0:n1, :]).bitcast(I32),
                in0=flat(w_top[g][:, n0:n1, :]).bitcast(I32),
                scalar1=HI_MASK,
                scalar2=None,
                op0=ALU.bitwise_and,
            )

        def sub(g, n0, n1):
            nc.vector.tensor_tensor(
                out=words_first(w_lo[g][:, n0:n1, :]),
                in0=rows_first(w_raw(g, n0, n1)),
                in1=words_first(w_hi[g][:, n0:n1, :]),
                op=ALU.subtract,
            )

        def quantize(codes, scales, values, c0, c1):
            nc.vector.quantize_mx(
                out=codes[:, c0:c1].bitcast(FP8X4), scales=scales[:, c0:c1], in_=values[:, PACK * c0 : PACK * c1]
            )

        def quantize_hi(g, n0, n1):
            quantize(hi_codes[g], hi_scales[g], flat(w_hi[g][:]), n0, n1)

        def quantize_lo(g, n0, n1):
            quantize(lo_codes[g], lo_scales[g], flat(w_lo[g][:]), n0, n1)

        def cast(a, g, m0, m1, engine):
            i = a * PASSES + g
            copy_on(
                engine,
                x_bf[i][:, :, m0:m1, :].rearrange("p r m j -> p m j r"),
                x_raw[a, g][:, :, PACK * m0 : PACK * m1].rearrange("p j (m r) -> p m j r", r=PACK),
            )

        def quantize_x(a, g, r0, r1):
            i = a * PASSES + g
            quantize(x_codes[i], x_scales[i], x_bf[i][:].rearrange("p r m j -> p (r m j)"), P * r0, P * r1)

        acc = {}

        def product(a, g, r, part):
            i = a * PASSES + g
            codes, scales = (hi_codes, hi_scales) if part == 0 else (lo_codes, lo_scales)
            if g == 0 and part == 0:
                acc[a, r] = psum.tile([P, M], F32, name="bank%d" % (PACK * a + r))
            nc.tensor.matmul_mx(
                out=acc[a, r][:],
                lhsT=x_codes[i][:, P * r : P * (r + 1)].bitcast(FP8X4),
                lhsT_scale=x_scales[i][:, P * r : P * (r + 1)],
                rhs=codes[g][:].bitcast(FP8X4),
                rhs_scale=scales[g][:],
                start=(g == 0 and part == 0),
                stop=(g == PASSES - 1 and part == 1),
            )

        def drain(a, r, n0, n1, engine):
            copy_on(engine, res[a][:, r, n0:n1], acc[a, r][:, n0:n1])

        def store_values(a, r0, r1):
            rows = out_0[a * T_HALF : (a + 1) * T_HALF, :]
            nc.sync.dma_start(out=rows.rearrange("(p r) n -> p r n", r=PACK)[:, r0:r1, :], in_=res[a][:, r0:r1, :])

        def interleave(a, n0, n1, engine):
            copy_on(engine, words_first(res_bf[a][:, n0:n1, :]), rows_first(res[a][:, :, n0:n1]))

        def quantize_res(a, n0, n1):
            quantize(res_codes[a], res_scales[:, a, :], flat(res_bf[a][:]), n0, n1)

        def store_words(a, n0, n1, queue):
            dst = out_1[a].rearrange("p n i -> p (n i)").bitcast(I32)
            queue.dma_start(out=dst[:, n0:n1], in_=res_codes[a][:, n0:n1].bitcast(I32))

        def store_scales(q, queue):
            queue.dma_start(
                out=out_2[:, 4 * q : 4 * q + 4, :].rearrange("a r n -> r a n").bitcast(I32),
                in_=res_scales[32 * q : 32 * q + 4, :, :].bitcast(I32),
            )

        def products(a, g):
            for part in range(2):
                for r in range(PACK):
                    product(a, g, r, part)

        def products_by_bank(a, g):
            for r in range(PACK):
                for part in range(2):
                    product(a, g, r, part)

        H, Q = N_HALF, N_HALF // 2
        load_w(0, 0, H)
        load_w(0, H, M)
        load_w(1, 0, M)
        load_x(0, 0, T, x_first[:])
        load_w(2, 0, M)
        load_x(1, 0, T_HALF, x_raw[0, 1])
        load_x(2, 0, T_HALF, x_raw[0, 2])
        load_x(1, T_HALF, T, x_raw[1, 1])
        load_x(2, T_HALF, T, x_raw[1, 2])

        top(0, 0, Q, "V")
        top(0, Q, H, "S")
        top(0, H, M, "S")
        mask(0, 0, Q)
        mask(0, Q, H)
        sub(0, 0, Q)
        quantize_hi(0, 0, H)
        sub(0, Q, H)
        mask(0, H, M)
        quantize_lo(0, 0, H)
        sub(0, H, M)
        top(1, 0, H, "S")
        top(1, H, M, "S")
        quantize_hi(0, H, M)
        mask(1, 0, H)
        quantize_lo(0, H, M)
        sub(1, 0, H)
        mask(1, H, M)
        quantize_lo(1, 0, H)
        quantize_hi(1, 0, H)
        cast(0, 0, 0, 48, "S")
        cast(0, 0, 48, P, "V")
        cast(1, 0, 0, P, "S")
        quantize_hi(1, H, M)
        quantize_x(0, 0, 0, PACK)
        products(0, 0)
        sub(1, H, M)
        top(2, 0, H, "V")
        top(2, H, M, "S")
        quantize_lo(1, H, M)
        mask(2, 0, H)
        quantize_x(1, 0, 0, PACK)
        products(1, 0)
        sub(2, 0, H)
        mask(2, H, M)
        cast(0, 1, 0, 112, "S")
        cast(0, 1, 112, P, "V")
        quantize_hi(2, 0, M)
        quantize_x(0, 1, 0, PACK)
        products(0, 1)
        cast(0, 2, 0, 112, "S")
        cast(0, 2, 112, P, "V")
        sub(2, H, M)
        quantize_x(0, 2, 0, PACK)
        quantize_lo(2, 0, M)
        for r0 in (0, 2):
            for part in range(2):
                for r in (r0, r0 + 1):
                    product(0, 2, r, part)
        cast(1, 1, 0, 80, "S")
        cast(1, 1, 80, P, "V")
        quantize_x(1, 1, 0, PACK)
        products(1, 1)
        drain(0, 0, 0, M, "S")
        store_values(0, 0, 1)
        drain(0, 1, 0, M, "S")
        store_values(0, 1, 2)
        drain(0, 2, 0, M, "S")
        drain(0, 3, 0, M, "S")
        store_values(0, 2, PACK)
        cast(1, 2, 0, P, "V")
        interleave(0, 0, H, "S")
        quantize_x(1, 2, 0, 2)
        quantize_x(1, 2, 2, PACK)
        products_by_bank(1, 2)
        interleave(0, H, M, "V")
        quantize_res(0, 0, M)
        store_words(0, 0, M, nc.sync)
        drain(1, 0, 0, M, "S")
        store_values(1, 0, 1)
        drain(1, 1, 0, M, "V")
        drain(1, 2, 0, M, "S")
        store_values(1, 1, 3)
        drain(1, 3, 0, H, "V")
        drain(1, 3, H, M, "S")
        store_values(1, 3, PACK)
        interleave(1, 0, H, "V")
        interleave(1, H + Q, M, "S")
        interleave(1, H, H + Q, "V")
        quantize_res(1, 0, H)
        store_words(1, 0, H, nc.scalar)
        quantize_res(1, H, M)
        store_words(1, H, M, nc.sync)
        for q in range(4):
            store_scales(q, nc.sync if q % 2 else nc.scalar)
